import numpy as np
import ml_dtypes


def mxq(x, axis, fmt="e4m3"):
    dtype, down = {"e4m3": (ml_dtypes.float8_e4m3fn, 7), "e5m2": (ml_dtypes.float8_e5m2, 14)}[fmt]
    v = np.moveaxis(np.asarray(x, np.float32).astype(ml_dtypes.bfloat16).astype(np.float64), axis, -1)
    blocks = v.reshape(v.shape[:-1] + (-1, 32))
    amax = np.abs(blocks).max(-1, keepdims=True)
    byte = np.maximum(np.where(amax > 0, np.frexp(amax)[1] - 1 + 127, 0) - down, 1)
    scale = np.exp2(byte - 127.0)
    codes = (blocks / scale).astype(np.float32).astype(dtype).astype(np.float64)
    return np.moveaxis((codes * scale).reshape(v.shape), -1, axis)


WIDE = False


def mx_kscale(k):
    if not WIDE:
        return np.ones(k)
    levels = np.array([10, -10, 5, -5, 0])
    if k % 512:
        return np.exp2(np.random.permutation(np.resize(levels, k // 32))).repeat(32)
    a = np.empty((k // 512, 16))
    for p in range(k // 512):
        a[p, :8] = np.random.permutation(np.resize(levels, 8))
        for g in range(8):
            far = levels[np.abs(levels - a[p, g]) >= 10]
            a[p, g + 8] = far[np.random.randint(len(far))]
    return np.exp2(a.ravel()).repeat(32)


def f64(x):
    return np.asarray(x).astype(np.float64)


def striped(idx):
    return np.tile(idx.reshape(-1, 16).T, (8, 1)).astype(np.uint16)


def unstriped(offs):
    return offs[:16].T.reshape(-1).astype(np.int64)


E2M1 = np.array([0.0, 0.5, 1.0, 1.5, 2.0, 3.0, 4.0, 6.0, -0.0, -0.5, -1.0, -1.5, -2.0, -3.0, -4.0, -6.0])


def pack_weight(w, fmt):
    k, n = w.shape
    w = f64(np.asarray(w, np.float32).astype(ml_dtypes.bfloat16)).reshape(k // 32, 32, n)
    amax = np.abs(w).max(1)
    if fmt == "e4m3":
        byte = np.frexp(amax)[1] - 1 + 127 - 7
    else:
        mant, ex = np.frexp(amax / 6.0)
        byte = np.where(mant > 0.5, ex, ex - 1) + 127
    byte = np.clip(np.where(amax > 0, byte, 1), 1, 254)
    scaled = (w * np.exp2(127.0 - byte)[:, None, :]).reshape(k, n).astype(np.float32)
    by_word = np.ascontiguousarray(scaled.reshape(k // 512, 128, 4, n).transpose(0, 1, 3, 2))
    if fmt == "e4m3":
        words = by_word.astype(ml_dtypes.float8_e4m3fn).view(np.uint8)
    else:
        c = by_word.astype(ml_dtypes.float4_e2m1fn).view(np.uint8) & 0xF
        words = (c[..., 0::2] | (c[..., 1::2] << 4)).reshape(k // 512, 128, 2 * n)
    return np.ascontiguousarray(words), np.ascontiguousarray(byte.astype(np.uint8).reshape(k // 512, 16, n))


def unpack_weight(words, scales, fmt):
    g, _, n = scales.shape
    words = np.ascontiguousarray(words).reshape(g, 128, n, -1)
    if fmt == "e4m3":
        vals = words.view(ml_dtypes.float8_e4m3fn).astype(np.float64)
    else:
        nib = np.empty((g, 128, n, 4), np.uint8)
        nib[..., 0::2] = words & 0xF
        nib[..., 1::2] = words >> 4
        vals = E2M1[nib]
    vals = vals * np.repeat(np.exp2(scales.astype(np.float64) - 127.0), 8, axis=1)[..., None]
    return vals.transpose(0, 1, 3, 2).reshape(g * 512, n)


def gelu(v):
    return 0.5 * v * (1.0 + np.tanh(np.sqrt(2.0 / np.pi) * (v + 0.044715 * v**3)))


K, T, S, H, T3, S2, P = 1536, 4096, 1024, 1024, 2048, 512, 512

def setup_inputs():
    n = np.random.standard_normal
    s = mx_kscale(K)[:, None]
    u = mx_kscale(H)[:, None]
    tab_words, tab_scales = pack_weight(n((K, T)) * s, "e4m3")
    tab2_words, tab2_scales = pack_weight(n((H, T3)) / np.sqrt(H) / u, "e4m3")
    w4_words, w4_scales = pack_weight(1.5 * n((H, S2)) / np.sqrt(H) / u, "e2m1")
    return {
        "tab_words": tab_words, "tab_scales": tab_scales,
        "offs": striped(np.random.permutation(T)[:S]),
        "tab2_words": tab2_words, "tab2_scales": tab2_scales,
        "offs2": striped(np.random.permutation(T3)[:S2]),
        "pos1": striped(np.random.permutation(S)[:P]),
        "pos2": striped(np.random.permutation(S)[:P]),
        "w1": (1.2 * n((K, H)) / np.sqrt(K) / s).astype(np.float32),
        "b1": (0.5 * n(H)).astype(np.float32),
        "gain": (np.random.uniform(0.6, 1.5, H) * u[:, 0]).astype(np.float32),
        "w4_words": w4_words, "w4_scales": w4_scales,
        "temp": np.random.uniform(0.4, 1.6, S2).astype(np.float32),
        "base": np.random.uniform(20.0, 100.0, S2).astype(np.float32),
    }

def reference(tab_words, tab_scales, offs, tab2_words, tab2_scales, offs2, pos1, pos2, w1, b1, gain, w4_words, w4_scales, temp, base):
    v = unpack_weight(tab_words, tab_scales, "e4m3")[:, unstriped(offs)]
    v2 = unpack_weight(tab2_words, tab2_scales, "e4m3")[:, unstriped(offs2)]
    w4 = unpack_weight(w4_words, w4_scales, "e2m1")
    h = f64(gain)[:, None] * np.tanh((mxq(f64(w1), 0, "e4m3").T @ v) + f64(b1)[:, None])
    hq = mxq(h, 0, "e4m3")
    e = v2.T @ hq
    d = w4.T @ hq
    top = e.max(axis=1)
    a = np.exp(f64(temp)[:, None] * (e[:, unstriped(pos1)] - top[:, None]))
    c = d[:, unstriped(pos2)]
    den = f64(base) + a.sum(axis=1)
    return a * c * (P / den)[:, None]

@@ -1,0 +1,343 @@
+from contextlib import ExitStack
+
+import concourse.mybir as mybir
+
+K, T, S, H, T3, S2, NP = 1536, 4096, 1024, 1024, 2048, 512, 512
+FLOPS = 2 * K * H * S + 2 * 2 * H * S2 * S
+
+F32 = mybir.dt.float32
+BF16 = mybir.dt.bfloat16
+I32 = mybir.dt.int32
+U32 = mybir.dt.uint32
+U16 = mybir.dt.uint16
+U8 = mybir.dt.uint8
+FP8X4 = mybir.dt.float8_e4m3fn_x4
+FP4X4 = mybir.dt.float4_e2m1fn_x4
+ALU = mybir.AluOpType
+ACT = mybir.ActivationFunctionType
+
+P = 128
+KP = K // 512
+HB = H // 512
+JQ = 256
+NQ = S // JQ
+MT = S2 // P
+VECTOR_SLOTS = {(0, 0): 0, (0, 1): 0, (0, 2): 3, (1, 0): 4, (1, 1): 0, (1, 2): 0}
+
+
+def tile_list_homologue_result_weighting_kernel(
+    tc, tab_words, tab_scales, offs, tab2_words, tab2_scales, offs2, pos1, pos2,
+    w1, b1, gain, w4_words, w4_scales, temp, base, out,
+):
+    nc = tc.nc
+    with ExitStack() as ctx:
+        lists = ctx.enter_context(tc.tile_pool(name="lists", bufs=1))
+        keep = ctx.enter_context(tc.tile_pool(name="keep", bufs=1))
+        ring = ctx.enter_context(tc.tile_pool(name="ring", bufs=1))
+        psum = ctx.enter_context(tc.psum_pool(name="psum", bufs=8))
+
+        idx = lists.tile([P, S // 16], U16, name="idx")
+        idx2 = lists.tile([P, S2 // 16], U16, name="idx2")
+        p1 = lists.tile([P, NP // 16], U16, name="p1")
+        p2 = lists.tile([P, NP // 16], U16, name="p2")
+
+        tab2_w = [keep.tile([P, T3], U32, name="tab2_w%d" % b) for b in range(HB)]
+        tab2_s = keep.tile([P, T3], U8, name="tab2_s")
+        w4_w = keep.tile([P, HB, 2 * S2], U8, name="w4_w", align_bytes=64)
+        w4_s = keep.tile([P, HB, S2], U8, name="w4_s", align_bytes=64)
+        v_w = [keep.tile([P, S], U32, name="v_w%d" % a, align_bytes=64) for a in range(KP)]
+        v_s = keep.tile([P, S], U8, name="v_s", align_bytes=64)
+        v2_w = [keep.tile([P, S2], U32, name="v2_w%d" % b, align_bytes=64) for b in range(HB)]
+        v2_s = keep.tile([P, S2], U8, name="v2_s", align_bytes=64)
+        w1_raw = {}
+        w1_w = {}
+        w1_s = {}
+        for b in range(HB):
+            for a in range(KP):
+                w1_raw[b, a] = keep.tile([P, 4, 512], F32, name="w1_raw%d%d" % (b, a))
+                w1_w[b, a] = keep.tile([P, 512], U32, name="w1_w%d%d" % (b, a), align_bytes=64)
+                w1_s[b, a] = keep.tile([P, 512], U8, name="w1_s%d%d" % (b, a), align_bytes=64)
+        h_w = {}
+        h_s = {}
+        for b in range(HB):
+            for half in range(2):
+                h_w[b, half] = keep.tile([P, 512], U32, name="h_w%d%d" % (b, half), align_bytes=64)
+                h_s[b, half] = keep.tile([P, 512], U8, name="h_s%d%d" % (b, half), align_bytes=64)
+        bias_sb = keep.tile([P, HB, 4], F32, name="bias_sb")
+        gain_sb = keep.tile([P, HB, 4], F32, name="gain_sb")
+        temp_sb = keep.tile([P, MT], F32, name="temp_sb")
+        base_sb = keep.tile([P, MT], F32, name="base_sb")
+        top0 = keep.tile([P, MT], F32, name="top0")
+        top = keep.tile([P, MT], F32, name="top")
+        shift = keep.tile([P, MT], F32, name="shift")
+        a_sum = keep.tile([P, MT], F32, name="a_sum")
+        den = keep.tile([P, MT], F32, name="den")
+        factor = keep.tile([P, MT], F32, name="factor")
+
+        def load_w1(b, a):
+            nc.sync.dma_start(
+                out=w1_raw[b, a][:],
+                in_=w1[512 * a : 512 * (a + 1), 512 * b : 512 * (b + 1)].rearrange("(p j) c -> p j c", j=4),
+            )
+
+        w1_bf = {}
+
+        def round_w1(b, a):
+            bf = ring.tile([P, 4, P, 4], BF16, name="w1_bf", bufs=3, align_bytes=64)
+            w1_bf[b, a] = bf
+            src = w1_raw[b, a][:].rearrange("p j (m t) -> p m j t", t=4)
+            dst = bf[:].rearrange("p t m j -> p m j t")
+            nv = VECTOR_SLOTS[b, a]
+            if nv > 0:
+                nc.vector.tensor_copy(out=dst[:, :, :, 0:nv], in_=src[:, :, :, 0:nv])
+            if nv < 4:
+                nc.scalar.copy(out=dst[:, :, :, nv:4], in_=src[:, :, :, nv:4])
+
+        def quantize_w1(b, a, parts):
+            flat = w1_bf[b, a][:].rearrange("p t m j -> p (t m j)")
+            words = 512 // parts
+            for u in range(parts):
+                nc.vector.quantize_mx(
+                    out=w1_w[b, a][:, u * words : (u + 1) * words].bitcast(FP8X4),
+                    scales=w1_s[b, a][:, u * words : (u + 1) * words],
+                    in_=flat[:, 4 * u * words : 4 * (u + 1) * words],
+                )
+
+        banks1 = {}
+
+        def first_pass(b, a):
+            for q in range(NQ):
+                for t in range(4):
+                    if a == 0 and t % 2 == 0:
+                        banks1[b, q, t // 2] = psum.tile([P, 2, JQ], F32, name="bank")
+                    nc.tensor.matmul_mx(
+                        out=banks1[b, q, t // 2][:, t % 2, :],
+                        lhsT=w1_w[b, a][:, P * t : P * (t + 1)].bitcast(FP8X4),
+                        lhsT_scale=w1_s[b, a][:, P * t : P * (t + 1)],
+                        rhs=v_w[a][:, JQ * q : JQ * (q + 1)].bitcast(FP8X4),
+                        rhs_scale=v_s[4 * a : P, JQ * q : JQ * (q + 1)],
+                        start=(a == 0 and t % 2 == 0),
+                        stop=(a == KP - 1 and t % 2 == 1),
+                    )
+
+        tanh_sb = {}
+        h_bf = {}
+
+        def tanh_step(b, q):
+            th = ring.tile([P, 4, JQ], F32, name="th", bufs=6)
+            tanh_sb[b, q] = th
+            for t in range(4):
+                nc.scalar.activation(
+                    out=th[:, t, :], in_=banks1[b, q, t // 2][:, t % 2, :], func=ACT.Tanh,
+                    bias=bias_sb[:, b, t : t + 1],
+                )
+
+        def gain_step(b, q):
+            hb = ring.tile([P, JQ, 4], BF16, name="hb", bufs=3, align_bytes=64)
+            h_bf[b, q] = hb
+            nc.vector.tensor_tensor(
+                out=hb[:].rearrange("p (c i) t -> p c t i", i=4),
+                in0=tanh_sb[b, q][:].rearrange("p t (c i) -> p c t i", i=4),
+                in1=gain_sb[:, b, :].unsqueeze(1).unsqueeze(3).broadcast_to([P, JQ // 4, 4, 4]),
+                op=ALU.mult,
+            )
+
+        def quantize_h(b, q):
+            cols = slice(JQ * (q % 2), JQ * (q % 2 + 1))
+            nc.vector.quantize_mx(
+                out=h_w[b, q // 2][:, cols].bitcast(FP8X4),
+                scales=h_s[b, q // 2][:, cols],
+                in_=h_bf[b, q][:].rearrange("p j t -> p (j t)"),
+            )
+
+        with tc.tile_pool(name="table", bufs=1) as table:
+            tab_w = [table.tile([P, T], U32, name="tab_w%d" % a) for a in range(KP)]
+            tab_s = table.tile([P, T], U8, name="tab_s")
+
+            nc.vector.memset(tab_s[:].bitcast(I32), 0)
+            nc.vector.memset(tab2_s[:].bitcast(I32), 0)
+            nc.vector.memset(w4_s[:].rearrange("p b c -> p (b c)").bitcast(I32), 0)
+
+            def load_table(a):
+                nc.sync.dma_start(
+                    out=tab_w[a][:].bitcast(I32),
+                    in_=tab_words[a].rearrange("p t i -> p (t i)").bitcast(I32),
+                )
+
+            nc.sync.dma_start(idx[:], offs)
+            load_table(0)
+            for quad in range(4):
+                nc.gpsimd.dma_start(
+                    out=tab_s[32 * quad : 32 * quad + 4 * KP, :].bitcast(I32),
+                    in_=tab_scales[:, 4 * quad : 4 * quad + 4, :].bitcast(I32),
+                )
+            nc.sync.dma_start(idx2[:], offs2)
+            nc.sync.dma_start(out=bias_sb[:], in_=b1.rearrange("(b p t) -> p b t", b=HB, t=4))
+            nc.sync.dma_start(out=gain_sb[:], in_=gain.rearrange("(b p t) -> p b t", b=HB, t=4))
+            for quad in range(4):
+                nc.gpsimd.dma_start(
+                    out=tab2_s[32 * quad : 32 * quad + 4 * HB, :].bitcast(I32),
+                    in_=tab2_scales[:, 4 * quad : 4 * quad + 4, :].bitcast(I32),
+                )
+            load_w1(0, 0)
+            load_table(1)
+            load_w1(0, 1)
+            load_table(2)
+            load_w1(0, 2)
+            load_w1(1, 0)
+            load_w1(1, 1)
+            load_w1(1, 2)
+            for b in range(HB):
+                nc.sync.dma_start(
+                    out=tab2_w[b][:].bitcast(I32),
+                    in_=tab2_words[b].rearrange("p t i -> p (t i)").bitcast(I32),
+                )
+            nc.sync.dma_start(
+                out=w4_w[:].bitcast(I32), in_=w4_words.rearrange("b p c -> p b c").bitcast(I32)
+            )
+            nc.sync.dma_start(p1[:], pos1)
+            nc.sync.dma_start(p2[:], pos2)
+            for quad in range(4):
+                nc.gpsimd.dma_start(
+                    out=w4_s[32 * quad : 32 * quad + 4, :, :].bitcast(I32),
+                    in_=w4_scales[:, 4 * quad : 4 * quad + 4, :].rearrange("b r c -> r b c").bitcast(I32),
+                )
+            with nc.allow_non_contiguous_dma(reason="one value a partition"):
+                nc.sync.dma_start(out=temp_sb[:], in_=temp.rearrange("(c p) -> p c", p=P))
+                nc.sync.dma_start(out=base_sb[:], in_=base.rearrange("(c p) -> p c", p=P))
+
+            for a in range(KP):
+                nc.vector.tensor_copy(v_w[a][:], tab_w[a][:].indirect(idx[:]))
+                if a == 0:
+                    nc.vector.tensor_copy(v_s[:], tab_s[:].indirect(idx[:]))
+                if a == 1:
+                    nc.vector.tensor_copy(v2_s[:], tab2_s[:].indirect(idx2[:]))
+                round_w1(0, a)
+                quantize_w1(0, a, 2 if a == KP - 1 else 1)
+                first_pass(0, a)
+
+        scores = ctx.enter_context(tc.tile_pool(name="scores", bufs=1))
+        e_sb = [scores.tile([P, S], F32, name="e_sb%d" % m) for m in range(MT)]
+        d_sb = [scores.tile([P, S], F32, name="d_sb%d" % m) for m in range(MT)]
+
+        for q in range(NQ):
+            tanh_step(0, q)
+        round_w1(1, 0)
+        quantize_w1(1, 0, 1)
+        round_w1(1, 1)
+        round_w1(1, 2)
+        for q in range(NQ):
+            gain_step(0, q)
+            if q > 0:
+                quantize_h(0, q - 1)
+        quantize_w1(1, 1, 1)
+        quantize_h(0, NQ - 1)
+        quantize_w1(1, 2, 2)
+        for a in range(KP):
+            first_pass(1, a)
+        for b in range(HB):
+            nc.vector.tensor_copy(v2_w[b][:], tab2_w[b][:].indirect(idx2[:]))
+        for q in range(NQ):
+            tanh_step(1, q)
+        for q in range(NQ):
+            gain_step(1, q)
+            if q > 0:
+                quantize_h(1, q - 1)
+        quantize_h(1, NQ - 1)
+
+        e_bank = {}
+        d_bank = {}
+
+        def second_products(m, half):
+            cols = slice(P * m, P * (m + 1))
+            e_bank[m, half] = psum.tile([P, 512], F32, name="bank")
+            for b in range(HB):
+                nc.tensor.matmul_mx(
+                    out=e_bank[m, half][:],
+                    lhsT=v2_w[b][:, cols].bitcast(FP8X4),
+                    lhsT_scale=v2_s[4 * b : P, cols],
+                    rhs=h_w[b, half][:].bitcast(FP8X4),
+                    rhs_scale=h_s[b, half][:],
+                    start=(b == 0),
+                    stop=(b == HB - 1),
+                )
+            d_bank[m, half] = psum.tile([P, 512], F32, name="bank")
+            for b in range(HB):
+                nc.tensor.matmul_mx(
+                    out=d_bank[m, half][:],
+                    lhsT=w4_w[:, b, 2 * P * m : 2 * P * (m + 1)].bitcast(FP4X4),
+                    lhsT_scale=w4_s[:, b, cols],
+                    rhs=h_w[b, half][:].bitcast(FP8X4),
+                    rhs_scale=h_s[b, half][:],
+                    start=(b == 0),
+                    stop=(b == HB - 1),
+                )
+
+        def copy_e(m, half):
+            nc.vector.tensor_scalar(
+                out=e_sb[m][:, 512 * half : 512 * (half + 1)], in0=e_bank[m, half][:],
+                scalar1=1.0, scalar2=(None if half == 0 else top0[:, m : m + 1]),
+                op0=ALU.mult, op1=ALU.max,
+                accum_out=(top0 if half == 0 else top)[:, m : m + 1],
+            )
+
+        def copy_d(m, half):
+            nc.scalar.copy(out=d_sb[m][:, 512 * half : 512 * (half + 1)], in_=d_bank[m, half][:])
+
+        a_sb = {}
+        a_full = {}
+        c_sb = {}
+
+        def look(m):
+            nc.vector.tensor_scalar(
+                out=shift[:, m : m + 1], in0=top[:, m : m + 1], scalar1=temp_sb[:, m : m + 1],
+                scalar2=-1.0, op0=ALU.mult, op1=ALU.mult,
+            )
+            a_sb[m] = scores.tile([P, NP], F32, name="a_sb%d" % m)
+            nc.scalar.activation(
+                out=a_sb[m][:], in_=e_sb[m][:].indirect(p1[:]), func=ACT.Exp,
+                bias=shift[:, m : m + 1], scale=temp_sb[:, m : m + 1],
+            )
+            a_full[m] = scores.tile([P, NP], F32, name="a_full%d" % m)
+            nc.scalar.activation(
+                out=a_full[m][:], in_=a_sb[m][:], func=ACT.Copy, scale=float(NP),
+                accum_out=a_sum[:, m : m + 1],
+            )
+
+        def pick(m):
+            c_sb[m] = scores.tile([P, NP], F32, name="c_sb%d" % m)
+            nc.vector.tensor_copy(c_sb[m][:], d_sb[m][:].indirect(p2[:]))
+
+        def normalise(m):
+            nc.vector.tensor_scalar(
+                out=den[:, m : m + 1], in0=a_sum[:, m : m + 1], scalar1=1.0 / NP,
+                scalar2=base_sb[:, m : m + 1], op0=ALU.mult, op1=ALU.add,
+            )
+            nc.vector.reciprocal(out=factor[:, m : m + 1], in_=den[:, m : m + 1])
+
+        def finish(m):
+            res = ring.tile([P, NP], F32, name="res", bufs=2)
+            nc.vector.scalar_tensor_tensor(
+                out=res[:], in0=a_full[m][:], scalar=factor[:, m : m + 1], in1=c_sb[m][:],
+                op0=ALU.mult, op1=ALU.mult,
+            )
+            nc.sync.dma_start(out=out[P * m : P * (m + 1), :], in_=res[:])
+
+        for m in range(MT):
+            second_products(m, 0)
+            copy_e(m, 0)
+            copy_d(m, 0)
+        for m in range(MT):
+            second_products(m, 1)
+            copy_e(m, 1)
+            copy_d(m, 1)
+            look(m)
+            if m > 0:
+                pick(m - 1)
+                normalise(m - 1)
+            if m > 1:
+                finish(m - 2)
+        pick(MT - 1)
+        finish(MT - 2)
+        normalise(MT - 1)
+        finish(MT - 1)

@@ -17,12 +17,14 @@ ALU = mybir.AluOpType
 ACT = mybir.ActivationFunctionType
 
 P = 128
-KP = K // 512
-HB = H // 512
-JQ = 256
-NQ = S // JQ
-MT = S2 // P
-VECTOR_SLOTS = {(0, 0): 0, (0, 1): 0, (0, 2): 3, (1, 0): 4, (1, 1): 0, (1, 2): 0}
+PASS = 512
+K_PASSES = K // PASS
+H_BLOCKS = H // PASS
+ROW_TILES = S2 // P
+STRIP = 256
+STRIPS = S // STRIP
+VECTOR_GROUPS = {(0, 2): 3, (1, 0): 4}
+A_PITCH = NP + 8
 
 
 def tile_list_homologue_result_weighting_kernel(
@@ -41,303 +43,269 @@ def tile_list_homologue_result_weighting_kernel(
         p1 = lists.tile([P, NP // 16], U16, name="p1")
         p2 = lists.tile([P, NP // 16], U16, name="p2")
 
-        tab2_w = [keep.tile([P, T3], U32, name="tab2_w%d" % b) for b in range(HB)]
+        tab2_w = [keep.tile([P, T3], U32, name="tab2_w%d" % b) for b in range(H_BLOCKS)]
         tab2_s = keep.tile([P, T3], U8, name="tab2_s")
-        w4_w = keep.tile([P, HB, 2 * S2], U8, name="w4_w", align_bytes=64)
-        w4_s = keep.tile([P, HB, S2], U8, name="w4_s", align_bytes=64)
-        v_w = [keep.tile([P, S], U32, name="v_w%d" % a, align_bytes=64) for a in range(KP)]
+        w4_w = keep.tile([P, H_BLOCKS, 2 * S2], U8, name="w4_w", align_bytes=64)
+        w4_s = keep.tile([P, H_BLOCKS, S2], U8, name="w4_s", align_bytes=64)
+        v_w = [keep.tile([P, S], U32, name="v_w%d" % a, align_bytes=64) for a in range(K_PASSES)]
         v_s = keep.tile([P, S], U8, name="v_s", align_bytes=64)
-        v2_w = [keep.tile([P, S2], U32, name="v2_w%d" % b, align_bytes=64) for b in range(HB)]
+        v2_w = [keep.tile([P, S2], U32, name="v2_w%d" % b, align_bytes=64) for b in range(H_BLOCKS)]
         v2_s = keep.tile([P, S2], U8, name="v2_s", align_bytes=64)
         w1_raw = {}
         w1_w = {}
         w1_s = {}
-        for b in range(HB):
-            for a in range(KP):
-                w1_raw[b, a] = keep.tile([P, 4, 512], F32, name="w1_raw%d%d" % (b, a))
-                w1_w[b, a] = keep.tile([P, 512], U32, name="w1_w%d%d" % (b, a), align_bytes=64)
-                w1_s[b, a] = keep.tile([P, 512], U8, name="w1_s%d%d" % (b, a), align_bytes=64)
+        for b in range(H_BLOCKS):
+            for a in range(K_PASSES):
+                w1_raw[b, a] = keep.tile([P, 4, PASS], F32, name="w1_raw%d%d" % (b, a))
+                w1_w[b, a] = keep.tile([P, PASS], U32, name="w1_w%d%d" % (b, a), align_bytes=64)
+                w1_s[b, a] = keep.tile([P, PASS], U8, name="w1_s%d%d" % (b, a), align_bytes=64)
         h_w = {}
         h_s = {}
-        for b in range(HB):
+        for b in range(H_BLOCKS):
             for half in range(2):
-                h_w[b, half] = keep.tile([P, 512], U32, name="h_w%d%d" % (b, half), align_bytes=64)
-                h_s[b, half] = keep.tile([P, 512], U8, name="h_s%d%d" % (b, half), align_bytes=64)
-        bias_sb = keep.tile([P, HB, 4], F32, name="bias_sb")
-        gain_sb = keep.tile([P, HB, 4], F32, name="gain_sb")
-        temp_sb = keep.tile([P, MT], F32, name="temp_sb")
-        base_sb = keep.tile([P, MT], F32, name="base_sb")
-        top0 = keep.tile([P, MT], F32, name="top0")
-        top = keep.tile([P, MT], F32, name="top")
-        shift = keep.tile([P, MT], F32, name="shift")
-        a_sum = keep.tile([P, MT], F32, name="a_sum")
-        den = keep.tile([P, MT], F32, name="den")
-        factor = keep.tile([P, MT], F32, name="factor")
+                h_w[b, half] = keep.tile([P, PASS], U32, name="h_w%d%d" % (b, half), align_bytes=64)
+                h_s[b, half] = keep.tile([P, PASS], U8, name="h_s%d%d" % (b, half), align_bytes=64)
+        bias_sb = keep.tile([P, H_BLOCKS, 4], F32, name="bias_sb")
+        gain_sb = keep.tile([P, H_BLOCKS, 4], F32, name="gain_sb")
+        temp_sb = keep.tile([P, ROW_TILES], F32, name="temp_sb")
+        a_sb = keep.tile([P, ROW_TILES, A_PITCH], F32, name="a_sb")
+        top_half = keep.tile([P, ROW_TILES], F32, name="top_half")
+        top = keep.tile([P, ROW_TILES], F32, name="top")
+        shift = keep.tile([P, ROW_TILES], F32, name="shift")
+        den = keep.tile([P, ROW_TILES], F32, name="den")
+        factor = keep.tile([P, ROW_TILES], F32, name="factor")
 
-        def load_w1(b, a):
+        def load_words(tile, words):
             nc.sync.dma_start(
-                out=w1_raw[b, a][:],
-                in_=w1[512 * a : 512 * (a + 1), 512 * b : 512 * (b + 1)].rearrange("(p j) c -> p j c", j=4),
+                out=tile[:].bitcast(I32), in_=words.rearrange("p t i -> p (t i)").bitcast(I32)
             )
 
-        w1_bf = {}
-
-        def round_w1(b, a):
-            bf = ring.tile([P, 4, P, 4], BF16, name="w1_bf", bufs=3, align_bytes=64)
-            w1_bf[b, a] = bf
-            src = w1_raw[b, a][:].rearrange("p j (m t) -> p m j t", t=4)
-            dst = bf[:].rearrange("p t m j -> p m j t")
-            nv = VECTOR_SLOTS[b, a]
-            if nv > 0:
-                nc.vector.tensor_copy(out=dst[:, :, :, 0:nv], in_=src[:, :, :, 0:nv])
-            if nv < 4:
-                nc.scalar.copy(out=dst[:, :, :, nv:4], in_=src[:, :, :, nv:4])
-
-        def quantize_w1(b, a, parts):
-            flat = w1_bf[b, a][:].rearrange("p t m j -> p (t m j)")
-            words = 512 // parts
-            for u in range(parts):
-                nc.vector.quantize_mx(
-                    out=w1_w[b, a][:, u * words : (u + 1) * words].bitcast(FP8X4),
-                    scales=w1_s[b, a][:, u * words : (u + 1) * words],
-                    in_=flat[:, 4 * u * words : 4 * (u + 1) * words],
+        def load_shared_scales(tile, scales, passes):
+            for quad in range(4):
+                nc.gpsimd.dma_start(
+                    out=tile[32 * quad : 32 * quad + 4 * passes, :].bitcast(I32),
+                    in_=scales[:, 4 * quad : 4 * quad + 4, :].bitcast(I32),
                 )
 
-        banks1 = {}
+        def load_w1(b, a):
+            rows = w1[PASS * a : PASS * (a + 1), PASS * b : PASS * (b + 1)]
+            nc.sync.dma_start(out=w1_raw[b, a][:], in_=rows.rearrange("(p j) c -> p j c", j=4))
 
-        def first_pass(b, a):
-            for q in range(NQ):
+        def quantize_w1(b, a):
+            rounded = ring.tile([P, 4, P, 4], BF16, name="w1_bf", bufs=3, align_bytes=64)
+            src = w1_raw[b, a][:].rearrange("p j (m t) -> p m j t", t=4)
+            dst = rounded[:].rearrange("p t m j -> p m j t")
+            split = VECTOR_GROUPS.get((b, a), 0)
+            if split > 0:
+                nc.vector.tensor_copy(out=dst[:, :, :, 0:split], in_=src[:, :, :, 0:split])
+            if split < 4:
+                nc.scalar.copy(out=dst[:, :, :, split:4], in_=src[:, :, :, split:4])
+            flat = rounded[:].rearrange("p t m j -> p (t m j)")
+            words = PASS // 2 if a == K_PASSES - 1 else PASS
+            for c0 in range(0, PASS, words):
+                nc.vector.quantize_mx(
+                    out=w1_w[b, a][:, c0 : c0 + words].bitcast(FP8X4),
+                    scales=w1_s[b, a][:, c0 : c0 + words],
+                    in_=flat[:, 4 * c0 : 4 * (c0 + words)],
+                )
+
+        h_bank = {}
+
+        def first_product(b, a):
+            for q in range(STRIPS):
+                cols = slice(STRIP * q, STRIP * (q + 1))
                 for t in range(4):
                     if a == 0 and t % 2 == 0:
-                        banks1[b, q, t // 2] = psum.tile([P, 2, JQ], F32, name="bank")
+                        h_bank[b, q, t // 2] = psum.tile([P, 2, STRIP], F32, name="bank")
                     nc.tensor.matmul_mx(
-                        out=banks1[b, q, t // 2][:, t % 2, :],
+                        out=h_bank[b, q, t // 2][:, t % 2, :],
                         lhsT=w1_w[b, a][:, P * t : P * (t + 1)].bitcast(FP8X4),
                         lhsT_scale=w1_s[b, a][:, P * t : P * (t + 1)],
-                        rhs=v_w[a][:, JQ * q : JQ * (q + 1)].bitcast(FP8X4),
-                        rhs_scale=v_s[4 * a : P, JQ * q : JQ * (q + 1)],
+                        rhs=v_w[a][:, cols].bitcast(FP8X4),
+                        rhs_scale=v_s[4 * a : P, cols],
                         start=(a == 0 and t % 2 == 0),
-                        stop=(a == KP - 1 and t % 2 == 1),
+                        stop=(a == K_PASSES - 1 and t % 2 == 1),
                     )
 
         tanh_sb = {}
         h_bf = {}
 
-        def tanh_step(b, q):
-            th = ring.tile([P, 4, JQ], F32, name="th", bufs=6)
-            tanh_sb[b, q] = th
+        def tanh_strip(b, q):
+            tanh_sb[b, q] = ring.tile([P, 4, STRIP], F32, name="tanh_sb", bufs=6)
             for t in range(4):
                 nc.scalar.activation(
-                    out=th[:, t, :], in_=banks1[b, q, t // 2][:, t % 2, :], func=ACT.Tanh,
+                    out=tanh_sb[b, q][:, t, :], in_=h_bank[b, q, t // 2][:, t % 2, :], func=ACT.Tanh,
                     bias=bias_sb[:, b, t : t + 1],
                 )
 
-        def gain_step(b, q):
-            hb = ring.tile([P, JQ, 4], BF16, name="hb", bufs=3, align_bytes=64)
-            h_bf[b, q] = hb
+        def gain_strip(b, q):
+            h_bf[b, q] = ring.tile([P, STRIP, 4], BF16, name="h_bf", bufs=3, align_bytes=64)
+            dst = h_bf[b, q][:].rearrange("p (c i) t -> p c t i", i=4)
             nc.vector.tensor_tensor(
-                out=hb[:].rearrange("p (c i) t -> p c t i", i=4),
+                out=dst,
                 in0=tanh_sb[b, q][:].rearrange("p t (c i) -> p c t i", i=4),
-                in1=gain_sb[:, b, :].unsqueeze(1).unsqueeze(3).broadcast_to([P, JQ // 4, 4, 4]),
+                in1=gain_sb[:, b, :].unsqueeze(1).unsqueeze(3).broadcast_to([P, STRIP // 4, 4, 4]),
                 op=ALU.mult,
             )
 
-        def quantize_h(b, q):
-            cols = slice(JQ * (q % 2), JQ * (q % 2 + 1))
+        def quantize_strip(b, q):
+            cols = slice(STRIP * (q % 2), STRIP * (q % 2 + 1))
             nc.vector.quantize_mx(
                 out=h_w[b, q // 2][:, cols].bitcast(FP8X4),
                 scales=h_s[b, q // 2][:, cols],
                 in_=h_bf[b, q][:].rearrange("p j t -> p (j t)"),
             )
 
+        def quantize_h(b):
+            for q in range(STRIPS):
+                gain_strip(b, q)
+                if q > 0:
+                    quantize_strip(b, q - 1)
+            quantize_strip(b, STRIPS - 1)
+
         with tc.tile_pool(name="table", bufs=1) as table:
-            tab_w = [table.tile([P, T], U32, name="tab_w%d" % a) for a in range(KP)]
+            tab_w = [table.tile([P, T], U32, name="tab_w%d" % a) for a in range(K_PASSES)]
             tab_s = table.tile([P, T], U8, name="tab_s")
 
             nc.vector.memset(tab_s[:].bitcast(I32), 0)
             nc.vector.memset(tab2_s[:].bitcast(I32), 0)
             nc.vector.memset(w4_s[:].rearrange("p b c -> p (b c)").bitcast(I32), 0)
 
-            def load_table(a):
-                nc.sync.dma_start(
-                    out=tab_w[a][:].bitcast(I32),
-                    in_=tab_words[a].rearrange("p t i -> p (t i)").bitcast(I32),
-                )
-
             nc.sync.dma_start(idx[:], offs)
-            load_table(0)
-            for quad in range(4):
-                nc.gpsimd.dma_start(
-                    out=tab_s[32 * quad : 32 * quad + 4 * KP, :].bitcast(I32),
-                    in_=tab_scales[:, 4 * quad : 4 * quad + 4, :].bitcast(I32),
-                )
+            load_words(tab_w[0], tab_words[0])
+            load_shared_scales(tab_s, tab_scales, K_PASSES)
             nc.sync.dma_start(idx2[:], offs2)
-            nc.sync.dma_start(out=bias_sb[:], in_=b1.rearrange("(b p t) -> p b t", b=HB, t=4))
-            nc.sync.dma_start(out=gain_sb[:], in_=gain.rearrange("(b p t) -> p b t", b=HB, t=4))
-            for quad in range(4):
-                nc.gpsimd.dma_start(
-                    out=tab2_s[32 * quad : 32 * quad + 4 * HB, :].bitcast(I32),
-                    in_=tab2_scales[:, 4 * quad : 4 * quad + 4, :].bitcast(I32),
-                )
+            nc.sync.dma_start(out=bias_sb[:], in_=b1.rearrange("(b p t) -> p b t", b=H_BLOCKS, t=4))
+            nc.sync.dma_start(out=gain_sb[:], in_=gain.rearrange("(b p t) -> p b t", b=H_BLOCKS, t=4))
+            load_shared_scales(tab2_s, tab2_scales, H_BLOCKS)
             load_w1(0, 0)
-            load_table(1)
-            load_w1(0, 1)
-            load_table(2)
-            load_w1(0, 2)
-            load_w1(1, 0)
-            load_w1(1, 1)
-            load_w1(1, 2)
-            for b in range(HB):
-                nc.sync.dma_start(
-                    out=tab2_w[b][:].bitcast(I32),
-                    in_=tab2_words[b].rearrange("p t i -> p (t i)").bitcast(I32),
-                )
+            for a in range(1, K_PASSES):
+                load_words(tab_w[a], tab_words[a])
+                load_w1(0, a)
+            for a in range(K_PASSES):
+                load_w1(1, a)
+            for b in range(H_BLOCKS):
+                load_words(tab2_w[b], tab2_words[b])
             nc.sync.dma_start(
                 out=w4_w[:].bitcast(I32), in_=w4_words.rearrange("b p c -> p b c").bitcast(I32)
             )
-            nc.sync.dma_start(p1[:], pos1)
-            nc.sync.dma_start(p2[:], pos2)
             for quad in range(4):
-                nc.gpsimd.dma_start(
+                nc.sync.dma_start(
                     out=w4_s[32 * quad : 32 * quad + 4, :, :].bitcast(I32),
                     in_=w4_scales[:, 4 * quad : 4 * quad + 4, :].rearrange("b r c -> r b c").bitcast(I32),
                 )
-            with nc.allow_non_contiguous_dma(reason="one value a partition"):
+            nc.sync.dma_start(p1[:], pos1)
+            nc.sync.dma_start(p2[:], pos2)
+            with nc.allow_non_contiguous_dma(reason="one value for each query, queries on the partitions"):
                 nc.sync.dma_start(out=temp_sb[:], in_=temp.rearrange("(c p) -> p c", p=P))
-                nc.sync.dma_start(out=base_sb[:], in_=base.rearrange("(c p) -> p c", p=P))
+                nc.sync.dma_start(out=a_sb[:, :, NP], in_=base.rearrange("(c p) -> p c", p=P))
 
-            for a in range(KP):
+            for a in range(K_PASSES):
                 nc.vector.tensor_copy(v_w[a][:], tab_w[a][:].indirect(idx[:]))
                 if a == 0:
                     nc.vector.tensor_copy(v_s[:], tab_s[:].indirect(idx[:]))
                 if a == 1:
                     nc.vector.tensor_copy(v2_s[:], tab2_s[:].indirect(idx2[:]))
-                round_w1(0, a)
-                quantize_w1(0, a, 2 if a == KP - 1 else 1)
-                first_pass(0, a)
+                quantize_w1(0, a)
+                first_product(0, a)
 
         scores = ctx.enter_context(tc.tile_pool(name="scores", bufs=1))
-        e_sb = [scores.tile([P, S], F32, name="e_sb%d" % m) for m in range(MT)]
-        d_sb = [scores.tile([P, S], F32, name="d_sb%d" % m) for m in range(MT)]
+        e_sb = [scores.tile([P, S], F32, name="e_sb%d" % c) for c in range(ROW_TILES)]
+        d_sb = [scores.tile([P, S], F32, name="d_sb%d" % c) for c in range(ROW_TILES)]
 
-        for q in range(NQ):
-            tanh_step(0, q)
-        round_w1(1, 0)
-        quantize_w1(1, 0, 1)
-        round_w1(1, 1)
-        round_w1(1, 2)
-        for q in range(NQ):
-            gain_step(0, q)
-            if q > 0:
-                quantize_h(0, q - 1)
-        quantize_w1(1, 1, 1)
-        quantize_h(0, NQ - 1)
-        quantize_w1(1, 2, 2)
-        for a in range(KP):
-            first_pass(1, a)
-        for b in range(HB):
+        for q in range(STRIPS):
+            tanh_strip(0, q)
+        for a in range(K_PASSES):
+            quantize_w1(1, a)
+        for a in range(K_PASSES):
+            first_product(1, a)
+        quantize_h(0)
+        for q in range(STRIPS):
+            tanh_strip(1, q)
+        for b in range(H_BLOCKS):
             nc.vector.tensor_copy(v2_w[b][:], tab2_w[b][:].indirect(idx2[:]))
-        for q in range(NQ):
-            tanh_step(1, q)
-        for q in range(NQ):
-            gain_step(1, q)
-            if q > 0:
-                quantize_h(1, q - 1)
-        quantize_h(1, NQ - 1)
+        quantize_h(1)
 
         e_bank = {}
         d_bank = {}
 
-        def second_products(m, half):
-            cols = slice(P * m, P * (m + 1))
-            e_bank[m, half] = psum.tile([P, 512], F32, name="bank")
-            for b in range(HB):
+        def second_products(c, half):
+            cols = slice(P * c, P * (c + 1))
+            e_bank[c, half] = psum.tile([P, PASS], F32, name="bank")
+            for b in range(H_BLOCKS):
                 nc.tensor.matmul_mx(
-                    out=e_bank[m, half][:],
+                    out=e_bank[c, half][:],
                     lhsT=v2_w[b][:, cols].bitcast(FP8X4),
                     lhsT_scale=v2_s[4 * b : P, cols],
                     rhs=h_w[b, half][:].bitcast(FP8X4),
                     rhs_scale=h_s[b, half][:],
                     start=(b == 0),
-                    stop=(b == HB - 1),
+                    stop=(b == H_BLOCKS - 1),
                 )
-            d_bank[m, half] = psum.tile([P, 512], F32, name="bank")
-            for b in range(HB):
+            d_bank[c, half] = psum.tile([P, PASS], F32, name="bank")
+            for b in range(H_BLOCKS):
                 nc.tensor.matmul_mx(
-                    out=d_bank[m, half][:],
-                    lhsT=w4_w[:, b, 2 * P * m : 2 * P * (m + 1)].bitcast(FP4X4),
+                    out=d_bank[c, half][:],
+                    lhsT=w4_w[:, b, 2 * P * c : 2 * P * (c + 1)].bitcast(FP4X4),
                     lhsT_scale=w4_s[:, b, cols],
                     rhs=h_w[b, half][:].bitcast(FP8X4),
                     rhs_scale=h_s[b, half][:],
                     start=(b == 0),
-                    stop=(b == HB - 1),
+                    stop=(b == H_BLOCKS - 1),
                 )
 
-        def copy_e(m, half):
+        def empty_banks(c, half):
+            cols = slice(PASS * half, PASS * (half + 1))
             nc.vector.tensor_scalar(
-                out=e_sb[m][:, 512 * half : 512 * (half + 1)], in0=e_bank[m, half][:],
-                scalar1=1.0, scalar2=(None if half == 0 else top0[:, m : m + 1]),
+                out=e_sb[c][:, cols], in0=e_bank[c, half][:], scalar1=1.0,
+                scalar2=(None if half == 0 else top_half[:, c : c + 1]),
                 op0=ALU.mult, op1=ALU.max,
-                accum_out=(top0 if half == 0 else top)[:, m : m + 1],
+                accum_out=(top_half if half == 0 else top)[:, c : c + 1],
             )
+            nc.scalar.copy(out=d_sb[c][:, cols], in_=d_bank[c, half][:])
 
-        def copy_d(m, half):
-            nc.scalar.copy(out=d_sb[m][:, 512 * half : 512 * (half + 1)], in_=d_bank[m, half][:])
+        a_small = {}
+        picked = {}
 
-        a_sb = {}
-        a_full = {}
-        c_sb = {}
-
-        def look(m):
+        def look(c):
             nc.vector.tensor_scalar(
-                out=shift[:, m : m + 1], in0=top[:, m : m + 1], scalar1=temp_sb[:, m : m + 1],
+                out=shift[:, c : c + 1], in0=top[:, c : c + 1], scalar1=temp_sb[:, c : c + 1],
                 scalar2=-1.0, op0=ALU.mult, op1=ALU.mult,
             )
-            a_sb[m] = scores.tile([P, NP], F32, name="a_sb%d" % m)
             nc.scalar.activation(
-                out=a_sb[m][:], in_=e_sb[m][:].indirect(p1[:]), func=ACT.Exp,
-                bias=shift[:, m : m + 1], scale=temp_sb[:, m : m + 1],
+                out=a_sb[:, c, 0:NP], in_=e_sb[c][:].indirect(p1[:]), func=ACT.Exp,
+                bias=shift[:, c : c + 1], scale=temp_sb[:, c : c + 1],
             )
-            a_full[m] = scores.tile([P, NP], F32, name="a_full%d" % m)
+            a_small[c] = ring.tile([P, NP + 1], F32, name="a_small", bufs=2)
             nc.scalar.activation(
-                out=a_full[m][:], in_=a_sb[m][:], func=ACT.Copy, scale=float(NP),
-                accum_out=a_sum[:, m : m + 1],
+                out=a_small[c][:], in_=a_sb[:, c, 0 : NP + 1], func=ACT.Copy, scale=1.0 / NP,
+                accum_out=den[:, c : c + 1],
             )
 
-        def pick(m):
-            c_sb[m] = scores.tile([P, NP], F32, name="c_sb%d" % m)
-            nc.vector.tensor_copy(c_sb[m][:], d_sb[m][:].indirect(p2[:]))
+        def pick(c):
+            picked[c] = scores.tile([P, NP], F32, name="picked%d" % c)
+            nc.vector.tensor_tensor(picked[c][:], d_sb[c][:].indirect(p2[:]), a_sb[:, c, 0:NP], ALU.mult)
 
-        def normalise(m):
-            nc.vector.tensor_scalar(
-                out=den[:, m : m + 1], in0=a_sum[:, m : m + 1], scalar1=1.0 / NP,
-                scalar2=base_sb[:, m : m + 1], op0=ALU.mult, op1=ALU.add,
-            )
-            nc.vector.reciprocal(out=factor[:, m : m + 1], in_=den[:, m : m + 1])
-
-        def finish(m):
+        def finish(c):
             res = ring.tile([P, NP], F32, name="res", bufs=2)
-            nc.vector.scalar_tensor_tensor(
-                out=res[:], in0=a_full[m][:], scalar=factor[:, m : m + 1], in1=c_sb[m][:],
-                op0=ALU.mult, op1=ALU.mult,
+            nc.vector.tensor_scalar(
+                out=res[:], in0=picked[c][:], scalar1=factor[:, c : c + 1], scalar2=None, op0=ALU.mult,
             )
-            nc.sync.dma_start(out=out[P * m : P * (m + 1), :], in_=res[:])
+            nc.sync.dma_start(out=out[P * c : P * (c + 1), :], in_=res[:])
 
-        for m in range(MT):
-            second_products(m, 0)
-            copy_e(m, 0)
-            copy_d(m, 0)
-        for m in range(MT):
-            second_products(m, 1)
-            copy_e(m, 1)
-            copy_d(m, 1)
-            look(m)
-            if m > 0:
-                pick(m - 1)
-                normalise(m - 1)
-            if m > 1:
-                finish(m - 2)
-        pick(MT - 1)
-        finish(MT - 2)
-        normalise(MT - 1)
-        finish(MT - 1)
+        for c in range(ROW_TILES):
+            second_products(c, 0)
+            empty_banks(c, 0)
+        for c in range(ROW_TILES):
+            second_products(c, 1)
+            empty_banks(c, 1)
+            look(c)
+            if c > 0:
+                pick(c - 1)
+                nc.vector.reciprocal(out=factor[:, c - 1 : c], in_=den[:, c - 1 : c])
+            if c > 1:
+                finish(c - 2)
+        pick(ROW_TILES - 1)
+        finish(ROW_TILES - 2)
+        nc.vector.reciprocal(out=factor[:, ROW_TILES - 1 :], in_=den[:, ROW_TILES - 1 :])
+        finish(ROW_TILES - 1)

from contextlib import ExitStack

import concourse.mybir as mybir

K, T, S, H, T3, S2, NP = 1536, 4096, 1024, 1024, 2048, 512, 512
FLOPS = 2 * K * H * S + 2 * 2 * H * S2 * S

F32 = mybir.dt.float32
BF16 = mybir.dt.bfloat16
I32 = mybir.dt.int32
U32 = mybir.dt.uint32
U16 = mybir.dt.uint16
U8 = mybir.dt.uint8
FP8X4 = mybir.dt.float8_e4m3fn_x4
FP4X4 = mybir.dt.float4_e2m1fn_x4
ALU = mybir.AluOpType
ACT = mybir.ActivationFunctionType

P = 128
PASS = 512
K_PASSES = K // PASS
H_BLOCKS = H // PASS
ROW_TILES = S2 // P
STRIP = 256
STRIPS = S // STRIP
VECTOR_GROUPS = {(0, 2): 3, (1, 0): 4}
A_PITCH = NP + 8


def tile_list_homologue_result_weighting_kernel(
    tc, tab_words, tab_scales, offs, tab2_words, tab2_scales, offs2, pos1, pos2,
    w1, b1, gain, w4_words, w4_scales, temp, base, out,
):
    nc = tc.nc
    with ExitStack() as ctx:
        lists = ctx.enter_context(tc.tile_pool(name="lists", bufs=1))
        keep = ctx.enter_context(tc.tile_pool(name="keep", bufs=1))
        ring = ctx.enter_context(tc.tile_pool(name="ring", bufs=1))
        psum = ctx.enter_context(tc.psum_pool(name="psum", bufs=8))

        idx = lists.tile([P, S // 16], U16, name="idx")
        idx2 = lists.tile([P, S2 // 16], U16, name="idx2")
        p1 = lists.tile([P, NP // 16], U16, name="p1")
        p2 = lists.tile([P, NP // 16], U16, name="p2")

        tab2_w = [keep.tile([P, T3], U32, name="tab2_w%d" % b) for b in range(H_BLOCKS)]
        tab2_s = keep.tile([P, T3], U8, name="tab2_s")
        w4_w = keep.tile([P, H_BLOCKS, 2 * S2], U8, name="w4_w", align_bytes=64)
        w4_s = keep.tile([P, H_BLOCKS, S2], U8, name="w4_s", align_bytes=64)
        v_w = [keep.tile([P, S], U32, name="v_w%d" % a, align_bytes=64) for a in range(K_PASSES)]
        v_s = keep.tile([P, S], U8, name="v_s", align_bytes=64)
        v2_w = [keep.tile([P, S2], U32, name="v2_w%d" % b, align_bytes=64) for b in range(H_BLOCKS)]
        v2_s = keep.tile([P, S2], U8, name="v2_s", align_bytes=64)
        w1_raw = {}
        w1_w = {}
        w1_s = {}
        for b in range(H_BLOCKS):
            for a in range(K_PASSES):
                w1_raw[b, a] = keep.tile([P, 4, PASS], F32, name="w1_raw%d%d" % (b, a))
                w1_w[b, a] = keep.tile([P, PASS], U32, name="w1_w%d%d" % (b, a), align_bytes=64)
                w1_s[b, a] = keep.tile([P, PASS], U8, name="w1_s%d%d" % (b, a), align_bytes=64)
        h_w = {}
        h_s = {}
        for b in range(H_BLOCKS):
            for half in range(2):
                h_w[b, half] = keep.tile([P, PASS], U32, name="h_w%d%d" % (b, half), align_bytes=64)
                h_s[b, half] = keep.tile([P, PASS], U8, name="h_s%d%d" % (b, half), align_bytes=64)
        bias_sb = keep.tile([P, H_BLOCKS, 4], F32, name="bias_sb")
        gain_sb = keep.tile([P, H_BLOCKS, 4], F32, name="gain_sb")
        temp_sb = keep.tile([P, ROW_TILES], F32, name="temp_sb")
        a_sb = keep.tile([P, ROW_TILES, A_PITCH], F32, name="a_sb")
        top_half = keep.tile([P, ROW_TILES], F32, name="top_half")
        top = keep.tile([P, ROW_TILES], F32, name="top")
        shift = keep.tile([P, ROW_TILES], F32, name="shift")
        den = keep.tile([P, ROW_TILES], F32, name="den")
        factor = keep.tile([P, ROW_TILES], F32, name="factor")

        def load_words(tile, words):
            nc.sync.dma_start(
                out=tile[:].bitcast(I32), in_=words.rearrange("p t i -> p (t i)").bitcast(I32)
            )

        def load_shared_scales(tile, scales, passes):
            for quad in range(4):
                nc.gpsimd.dma_start(
                    out=tile[32 * quad : 32 * quad + 4 * passes, :].bitcast(I32),
                    in_=scales[:, 4 * quad : 4 * quad + 4, :].bitcast(I32),
                )

        def load_w1(b, a):
            rows = w1[PASS * a : PASS * (a + 1), PASS * b : PASS * (b + 1)]
            nc.sync.dma_start(out=w1_raw[b, a][:], in_=rows.rearrange("(p j) c -> p j c", j=4))

        def quantize_w1(b, a):
            rounded = ring.tile([P, 4, P, 4], BF16, name="w1_bf", bufs=3, align_bytes=64)
            src = w1_raw[b, a][:].rearrange("p j (m t) -> p m j t", t=4)
            dst = rounded[:].rearrange("p t m j -> p m j t")
            split = VECTOR_GROUPS.get((b, a), 0)
            if split > 0:
                nc.vector.tensor_copy(out=dst[:, :, :, 0:split], in_=src[:, :, :, 0:split])
            if split < 4:
                nc.scalar.copy(out=dst[:, :, :, split:4], in_=src[:, :, :, split:4])
            flat = rounded[:].rearrange("p t m j -> p (t m j)")
            words = PASS // 2 if a == K_PASSES - 1 else PASS
            for c0 in range(0, PASS, words):
                nc.vector.quantize_mx(
                    out=w1_w[b, a][:, c0 : c0 + words].bitcast(FP8X4),
                    scales=w1_s[b, a][:, c0 : c0 + words],
                    in_=flat[:, 4 * c0 : 4 * (c0 + words)],
                )

        h_bank = {}

        def first_product(b, a):
            for q in range(STRIPS):
                cols = slice(STRIP * q, STRIP * (q + 1))
                for t in range(4):
                    if a == 0 and t % 2 == 0:
                        h_bank[b, q, t // 2] = psum.tile([P, 2, STRIP], F32, name="bank")
                    nc.tensor.matmul_mx(
                        out=h_bank[b, q, t // 2][:, t % 2, :],
                        lhsT=w1_w[b, a][:, P * t : P * (t + 1)].bitcast(FP8X4),
                        lhsT_scale=w1_s[b, a][:, P * t : P * (t + 1)],
                        rhs=v_w[a][:, cols].bitcast(FP8X4),
                        rhs_scale=v_s[4 * a : P, cols],
                        start=(a == 0 and t % 2 == 0),
                        stop=(a == K_PASSES - 1 and t % 2 == 1),
                    )

        tanh_sb = {}
        h_bf = {}

        def tanh_strip(b, q):
            tanh_sb[b, q] = ring.tile([P, 4, STRIP], F32, name="tanh_sb", bufs=6)
            for t in range(4):
                nc.scalar.activation(
                    out=tanh_sb[b, q][:, t, :], in_=h_bank[b, q, t // 2][:, t % 2, :], func=ACT.Tanh,
                    bias=bias_sb[:, b, t : t + 1],
                )

        def gain_strip(b, q):
            h_bf[b, q] = ring.tile([P, STRIP, 4], BF16, name="h_bf", bufs=3, align_bytes=64)
            dst = h_bf[b, q][:].rearrange("p (c i) t -> p c t i", i=4)
            nc.vector.tensor_tensor(
                out=dst,
                in0=tanh_sb[b, q][:].rearrange("p t (c i) -> p c t i", i=4),
                in1=gain_sb[:, b, :].unsqueeze(1).unsqueeze(3).broadcast_to([P, STRIP // 4, 4, 4]),
                op=ALU.mult,
            )

        def quantize_strip(b, q):
            cols = slice(STRIP * (q % 2), STRIP * (q % 2 + 1))
            nc.vector.quantize_mx(
                out=h_w[b, q // 2][:, cols].bitcast(FP8X4),
                scales=h_s[b, q // 2][:, cols],
                in_=h_bf[b, q][:].rearrange("p j t -> p (j t)"),
            )

        def quantize_h(b):
            for q in range(STRIPS):
                gain_strip(b, q)
                if q > 0:
                    quantize_strip(b, q - 1)
            quantize_strip(b, STRIPS - 1)

        with tc.tile_pool(name="table", bufs=1) as table:
            tab_w = [table.tile([P, T], U32, name="tab_w%d" % a) for a in range(K_PASSES)]
            tab_s = table.tile([P, T], U8, name="tab_s")

            nc.vector.memset(tab_s[:].bitcast(I32), 0)
            nc.vector.memset(tab2_s[:].bitcast(I32), 0)
            nc.vector.memset(w4_s[:].rearrange("p b c -> p (b c)").bitcast(I32), 0)

            nc.sync.dma_start(idx[:], offs)
            load_words(tab_w[0], tab_words[0])
            load_shared_scales(tab_s, tab_scales, K_PASSES)
            nc.sync.dma_start(idx2[:], offs2)
            nc.sync.dma_start(out=bias_sb[:], in_=b1.rearrange("(b p t) -> p b t", b=H_BLOCKS, t=4))
            nc.sync.dma_start(out=gain_sb[:], in_=gain.rearrange("(b p t) -> p b t", b=H_BLOCKS, t=4))
            load_shared_scales(tab2_s, tab2_scales, H_BLOCKS)
            load_w1(0, 0)
            for a in range(1, K_PASSES):
                load_words(tab_w[a], tab_words[a])
                load_w1(0, a)
            for a in range(K_PASSES):
                load_w1(1, a)
            for b in range(H_BLOCKS):
                load_words(tab2_w[b], tab2_words[b])
            nc.sync.dma_start(
                out=w4_w[:].bitcast(I32), in_=w4_words.rearrange("b p c -> p b c").bitcast(I32)
            )
            for quad in range(4):
                nc.sync.dma_start(
                    out=w4_s[32 * quad : 32 * quad + 4, :, :].bitcast(I32),
                    in_=w4_scales[:, 4 * quad : 4 * quad + 4, :].rearrange("b r c -> r b c").bitcast(I32),
                )
            nc.sync.dma_start(p1[:], pos1)
            nc.sync.dma_start(p2[:], pos2)
            with nc.allow_non_contiguous_dma(reason="one value for each query, queries on the partitions"):
                nc.sync.dma_start(out=temp_sb[:], in_=temp.rearrange("(c p) -> p c", p=P))
                nc.sync.dma_start(out=a_sb[:, :, NP], in_=base.rearrange("(c p) -> p c", p=P))

            for a in range(K_PASSES):
                nc.vector.tensor_copy(v_w[a][:], tab_w[a][:].indirect(idx[:]))
                if a == 0:
                    nc.vector.tensor_copy(v_s[:], tab_s[:].indirect(idx[:]))
                if a == 1:
                    nc.vector.tensor_copy(v2_s[:], tab2_s[:].indirect(idx2[:]))
                quantize_w1(0, a)
                first_product(0, a)

        scores = ctx.enter_context(tc.tile_pool(name="scores", bufs=1))
        e_sb = [scores.tile([P, S], F32, name="e_sb%d" % c) for c in range(ROW_TILES)]
        d_sb = [scores.tile([P, S], F32, name="d_sb%d" % c) for c in range(ROW_TILES)]

        for q in range(STRIPS):
            tanh_strip(0, q)
        for a in range(K_PASSES):
            quantize_w1(1, a)
        for a in range(K_PASSES):
            first_product(1, a)
        quantize_h(0)
        for q in range(STRIPS):
            tanh_strip(1, q)
        for b in range(H_BLOCKS):
            nc.vector.tensor_copy(v2_w[b][:], tab2_w[b][:].indirect(idx2[:]))
        quantize_h(1)

        e_bank = {}
        d_bank = {}

        def second_products(c, half):
            cols = slice(P * c, P * (c + 1))
            e_bank[c, half] = psum.tile([P, PASS], F32, name="bank")
            for b in range(H_BLOCKS):
                nc.tensor.matmul_mx(
                    out=e_bank[c, half][:],
                    lhsT=v2_w[b][:, cols].bitcast(FP8X4),
                    lhsT_scale=v2_s[4 * b : P, cols],
                    rhs=h_w[b, half][:].bitcast(FP8X4),
                    rhs_scale=h_s[b, half][:],
                    start=(b == 0),
                    stop=(b == H_BLOCKS - 1),
                )
            d_bank[c, half] = psum.tile([P, PASS], F32, name="bank")
            for b in range(H_BLOCKS):
                nc.tensor.matmul_mx(
                    out=d_bank[c, half][:],
                    lhsT=w4_w[:, b, 2 * P * c : 2 * P * (c + 1)].bitcast(FP4X4),
                    lhsT_scale=w4_s[:, b, cols],
                    rhs=h_w[b, half][:].bitcast(FP8X4),
                    rhs_scale=h_s[b, half][:],
                    start=(b == 0),
                    stop=(b == H_BLOCKS - 1),
                )

        def empty_banks(c, half):
            cols = slice(PASS * half, PASS * (half + 1))
            nc.vector.tensor_scalar(
                out=e_sb[c][:, cols], in0=e_bank[c, half][:], scalar1=1.0,
                scalar2=(None if half == 0 else top_half[:, c : c + 1]),
                op0=ALU.mult, op1=ALU.max,
                accum_out=(top_half if half == 0 else top)[:, c : c + 1],
            )
            nc.scalar.copy(out=d_sb[c][:, cols], in_=d_bank[c, half][:])

        a_small = {}
        picked = {}

        def look(c):
            nc.vector.tensor_scalar(
                out=shift[:, c : c + 1], in0=top[:, c : c + 1], scalar1=temp_sb[:, c : c + 1],
                scalar2=-1.0, op0=ALU.mult, op1=ALU.mult,
            )
            nc.scalar.activation(
                out=a_sb[:, c, 0:NP], in_=e_sb[c][:].indirect(p1[:]), func=ACT.Exp,
                bias=shift[:, c : c + 1], scale=temp_sb[:, c : c + 1],
            )
            a_small[c] = ring.tile([P, NP + 1], F32, name="a_small", bufs=2)
            nc.scalar.activation(
                out=a_small[c][:], in_=a_sb[:, c, 0 : NP + 1], func=ACT.Copy, scale=1.0 / NP,
                accum_out=den[:, c : c + 1],
            )

        def pick(c):
            picked[c] = scores.tile([P, NP], F32, name="picked%d" % c)
            nc.vector.tensor_tensor(picked[c][:], d_sb[c][:].indirect(p2[:]), a_sb[:, c, 0:NP], ALU.mult)

        def finish(c):
            res = ring.tile([P, NP], F32, name="res", bufs=2)
            nc.vector.tensor_scalar(
                out=res[:], in0=picked[c][:], scalar1=factor[:, c : c + 1], scalar2=None, op0=ALU.mult,
            )
            nc.sync.dma_start(out=out[P * c : P * (c + 1), :], in_=res[:])

        for c in range(ROW_TILES):
            second_products(c, 0)
            empty_banks(c, 0)
        for c in range(ROW_TILES):
            second_products(c, 1)
            empty_banks(c, 1)
            look(c)
            if c > 0:
                pick(c - 1)
                nc.vector.reciprocal(out=factor[:, c - 1 : c], in_=den[:, c - 1 : c])
            if c > 1:
                finish(c - 2)
        pick(ROW_TILES - 1)
        finish(ROW_TILES - 2)
        nc.vector.reciprocal(out=factor[:, ROW_TILES - 1 :], in_=den[:, ROW_TILES - 1 :])
        finish(ROW_TILES - 1)
